import numpy as np
import ml_dtypes


def mxq(x, axis, fmt="e4m3"):
    dtype, down = {"e4m3": (ml_dtypes.float8_e4m3fn, 7), "e5m2": (ml_dtypes.float8_e5m2, 14)}[fmt]
    v = np.moveaxis(np.asarray(x, np.float32).astype(ml_dtypes.bfloat16).astype(np.float64), axis, -1)
    blocks = v.reshape(v.shape[:-1] + (-1, 32))
    amax = np.abs(blocks).max(-1, keepdims=True)
    byte = np.maximum(np.where(amax > 0, np.frexp(amax)[1] - 1 + 127, 0) - down, 1)
    scale = np.exp2(byte - 127.0)
    codes = (blocks / scale).astype(np.float32).astype(dtype).astype(np.float64)
    return np.moveaxis((codes * scale).reshape(v.shape), -1, axis)


WIDE = False


def mx_kscale(k):
    if not WIDE:
        return np.ones(k)
    levels = np.array([10, -10, 5, -5, 0])
    if k % 512:
        return np.exp2(np.random.permutation(np.resize(levels, k // 32))).repeat(32)
    a = np.empty((k // 512, 16))
    for p in range(k // 512):
        a[p, :8] = np.random.permutation(np.resize(levels, 8))
        for g in range(8):
            far = levels[np.abs(levels - a[p, g]) >= 10]
            a[p, g + 8] = far[np.random.randint(len(far))]
    return np.exp2(a.ravel()).repeat(32)


def f64(x):
    return np.asarray(x).astype(np.float64)


def striped(idx):
    return np.tile(idx.reshape(-1, 16).T, (8, 1)).astype(np.uint16)


def unstriped(offs):
    return offs[:16].T.reshape(-1).astype(np.int64)


def striped8(idx):
    return np.concatenate([x.reshape(-1, 16).T for x in idx]).astype(np.uint16)


def runs(offs, k):
    lists = np.stack([offs[16 * r : 16 * r + 16].T.reshape(-1) for r in range(8)]).astype(np.int64)
    return lists[np.arange(k) % 512 // 64]


def pack_weight(w):
    k, n = w.shape
    w = f64(np.asarray(w, np.float32).astype(ml_dtypes.bfloat16)).reshape(k // 32, 32, n)
    amax = np.abs(w).max(1)
    byte = np.clip(np.where(amax > 0, np.frexp(amax)[1] - 1 + 127 - 7, 1), 1, 254)
    scaled = (w * np.exp2(127.0 - byte)[:, None, :]).reshape(k, n).astype(np.float32)
    words = np.ascontiguousarray(scaled.reshape(k // 512, 128, 4, n).transpose(0, 1, 3, 2)).astype(ml_dtypes.float8_e4m3fn).view(np.uint8)
    return words, np.ascontiguousarray(byte.astype(np.uint8).reshape(k // 512, 16, n))


def unpack_weight(words, scales):
    g, p, n, _ = words.shape
    vals = np.ascontiguousarray(words).view(ml_dtypes.float8_e4m3fn).astype(np.float64) * np.repeat(np.exp2(scales.astype(np.float64) - 127.0), 8, axis=1)[..., None]
    return vals.transpose(0, 1, 3, 2).reshape(g * 512, n)


def sigmoid(v):
    return 1.0 / (1.0 + np.exp(-np.maximum(v, -700.0)))

def planes(y):
    n, m = y.shape
    v = y.astype(np.float32).astype(ml_dtypes.bfloat16).astype(np.float64).reshape(n // 32, 32, m)
    top = np.abs(v).max(1)
    byte = np.clip(np.where(top > 0, np.frexp(top)[1] - 1 + 127 - 7, 1), 1, 254)
    codes = (v * np.exp2(127.0 - byte)[:, None, :]).reshape(n, m).astype(np.float32).astype(ml_dtypes.float8_e4m3fn).view(np.uint8)
    words = codes.reshape(n // 512, 128, 4, m).transpose(0, 1, 3, 2)
    return np.ascontiguousarray(words), np.ascontiguousarray(byte.astype(np.uint8).reshape(n // 512, 16, m))


K, T, S, N, H = 512, 2048, 512, 512, 512


def setup_inputs():
    n = np.random.standard_normal
    s = mx_kscale(K)[:, None]
    u = mx_kscale(H)
    packed_xT = pack_weight(n((K, T)) * s)
    packed_w1 = pack_weight(n((K, H)) / np.sqrt(K) / s)
    packed_w2 = pack_weight(n((H, N)) / np.sqrt(H) / u[:, None])
    packed_w3 = pack_weight(n((K, N)) / np.sqrt(K) / s)
    return {
        "x_words": packed_xT[0],
        "x_scales": packed_xT[1],
        "w1_words": packed_w1[0],
        "w1_scales": packed_w1[1],
        "gn": (np.random.uniform(0.5, 1.5, (H, 1)) * u[:, None]).astype(np.float32),
        "w2_words": packed_w2[0],
        "w2_scales": packed_w2[1],
        "w3_words": packed_w3[0],
        "w3_scales": packed_w3[1],
        "offs": striped(np.random.permutation(T)[:S]),
        "n1": striped8(np.stack([np.random.permutation(S) for _ in range(8)])),
        "n2": striped8(np.stack([np.random.permutation(S) for _ in range(8)])),
        "two": striped(np.random.permutation(T)[:S]),
        "n3": striped8(np.stack([np.random.permutation(S) for _ in range(8)])),
        "n4": striped8(np.stack([np.random.permutation(S) for _ in range(8)])),
    }


def reference(x_words, x_scales, w1_words, w1_scales, gn, w2_words, w2_scales, w3_words, w3_scales, offs, n1, n2, two, n3, n4):
    xq = unpack_weight(x_words, x_scales)[:, unstriped(offs)]
    y = unpack_weight(w1_words, w1_scales).T @ xq
    ex = np.exp(0.5 * y)
    z = f64(gn) * ((2.0 * ex) / (ex + ex[np.arange(H)[:, None], runs(n1, H)] + ex[np.arange(H)[:, None], runs(n2, H)]))
    h = unpack_weight(w2_words, w2_scales).T @ mxq(z, 0, "e4m3")
    x_two = unpack_weight(x_words, x_scales)[:, unstriped(two)]
    d = unpack_weight(w3_words, w3_scales).T @ x_two
    out_0 = (h + h[np.arange(N)[:, None], runs(n3, N)]) * (sigmoid(d + d[np.arange(N)[:, None], runs(n4, N)]))
    return (out_0,) + planes(out_0)

@@ -1,0 +1,216 @@
+from contextlib import ExitStack
+
+import concourse.mybir as mybir
+
+K, T, S, N, H = 512, 2048, 512, 512, 512
+FLOPS = 3 * 2 * 512 * 512 * 512
+
+F32 = mybir.dt.float32
+BF16 = mybir.dt.bfloat16
+I32 = mybir.dt.int32
+U32 = mybir.dt.uint32
+U16 = mybir.dt.uint16
+U8 = mybir.dt.uint8
+FP8X4 = mybir.dt.float8_e4m3fn_x4
+ACT = mybir.ActivationFunctionType
+ALU = mybir.AluOpType
+
+P = 128
+PACK = 4
+HALF = S // 2
+SCALAR_SLOTS = (3,)
+OUT_PIECES = ((0, 256), (256, 384), (384, 512))
+
+
+def tile_picked_latetriebshare_none_po_kernel(
+    tc, x_words, x_scales, w1_words, w1_scales, gn, w2_words, w2_scales, w3_words, w3_scales,
+    offs, n1, n2, two, n3, n4, out_0, out_1, out_2,
+):
+    nc = tc.nc
+    with ExitStack() as ctx:
+        keep = ctx.enter_context(tc.tile_pool(name="keep", bufs=1))
+        psum = ctx.enter_context(tc.psum_pool(name="psum", bufs=1))
+
+        def sb(name, shape, dtype, tag=None):
+            return keep.tile(shape, dtype, name=name, tag=tag or name, align_bytes=64)
+
+        def load_list(name, src):
+            t = sb(name, [P, S // 16], U16)
+            nc.sync.dma_start(t[:], src)
+            return t
+
+        def load_words(queue, name, src, width):
+            t = sb(name, [P, width], I32)
+            queue.dma_start(t[:], src[0].rearrange("p c r -> p (c r)").bitcast(I32))
+            return t
+
+        def load_scales(plane, src, queues):
+            for q in range(4):
+                queues[q % 2].dma_start(
+                    plane[32 * q : 32 * q + 4, :].bitcast(I32),
+                    src[0, 4 * q : 4 * q + 4, :].bitcast(I32),
+                )
+
+        def piece(lst, c):
+            return lst[:, c * (HALF // 16) : (c + 1) * (HALF // 16)]
+
+        def cols(c):
+            return slice(c * HALF, (c + 1) * HALF)
+
+        def deal(name, raw, dtype, tag=None):
+            t = sb(name, [P, PACK, P], dtype, tag)
+            nc.vector.tensor_copy(t[:].rearrange("p t m -> p m t"), raw[:].rearrange("p (m t) -> p m t", t=PACK))
+            return t
+
+        xs_raw = sb("xs_raw", [P, T], U8)
+        w1s_raw = sb("w1s_raw", [P, H], U8)
+        w3s_raw = sb("w3s_raw", [P, N], U8)
+        w2s_raw = sb("w2s_raw", [P, N], U8)
+        nc.vector.memset(xs_raw[:].bitcast(I32), 0)
+        for plane in (w1s_raw, w3s_raw, w2s_raw):
+            nc.gpsimd.memset(plane[:].bitcast(I32), 0)
+
+        offs_t = load_list("offs_t", offs)
+        two_t = load_list("two_t", two)
+        load_scales(xs_raw, x_scales, (nc.sync, nc.scalar))
+        w1w_raw = load_words(nc.sync, "w1w_raw", w1_words, H)
+        xw_raw = load_words(nc.sync, "xw_raw", x_words, T)
+        load_scales(w1s_raw, w1_scales, (nc.sync, nc.sync))
+        w3w_raw = load_words(nc.sync, "w3w_raw", w3_words, N)
+        n1_t = load_list("n1_t", n1)
+        n2_t = load_list("n2_t", n2)
+        n4_t = load_list("n4_t", n4)
+        w2w_raw = load_words(nc.sync, "w2w_raw", w2_words, N)
+        n3_t = load_list("n3_t", n3)
+        load_scales(w3s_raw, w3_scales, (nc.gpsimd, nc.gpsimd))
+        load_scales(w2s_raw, w2_scales, (nc.gpsimd, nc.gpsimd))
+        gain = sb("gain", [P, PACK], F32)
+        nc.gpsimd.dma_start(gain[:], gn.rearrange("(p t) o -> p (t o)", t=PACK))
+
+        def pick_scales(name, lst):
+            t = sb(name, [P, S], U8)
+            nc.vector.tensor_copy(t[:], xs_raw[:].indirect(lst[:]))
+            return t
+
+        def pick_words(name, lst, tag=None):
+            t = sb(name, [P, S], I32, tag)
+            nc.vector.tensor_copy(t[:].bitcast(U32), xw_raw[:].bitcast(U32).indirect(lst[:]))
+            return t
+
+        xa_s = pick_scales("xa_s", offs_t)
+        w1w = deal("w1w", w1w_raw, I32)
+        xb_s = pick_scales("xb_s", two_t)
+        xa_w = pick_words("xa_w", offs_t)
+        w1s = deal("w1s", w1s_raw, U8)
+        xb_w = pick_words("xb_w", two_t, "w1s_raw")
+        w3w = deal("w3w", w3w_raw, I32)
+        w3s = deal("w3s", w3s_raw, U8, "w3w_raw")
+
+        def product(bank, ww, ws, t, xw, xs):
+            nc.tensor.matmul_mx(
+                out=bank, lhsT=ww[:, t, :].bitcast(FP8X4), lhsT_scale=ws[:, t, :],
+                rhs=xw.bitcast(FP8X4), rhs_scale=xs, start=True, stop=True,
+            )
+
+        y_ps = [psum.tile([P, S], F32, name=f"y_ps{t}", tag=f"lo{t}") for t in range(PACK)]
+        d_ps = [psum.tile([P, S], F32, name=f"d_ps{t}", tag=f"hi{t}") for t in range(PACK)]
+        for t in range(PACK):
+            product(y_ps[t][:], w1w, w1s, t, xa_w[:], xa_s[:])
+        for t in range(PACK):
+            product(d_ps[t][:], w3w, w3s, t, xb_w[:], xb_s[:])
+
+        win = [sb(f"win{t}", [P, S], F32) for t in range(PACK)]
+        e1 = [sb(f"e1_{t}", [P, S], F32) for t in range(PACK)]
+        e2 = [sb(f"e2_{t}", [P, S], F32) for t in SCALAR_SLOTS]
+        pair = [sb(f"pair{t}", [P, S], F32) for t in range(PACK)]
+        for t in range(PACK):
+            if t in SCALAR_SLOTS:
+                nc.scalar.copy(win[t][:], y_ps[t][:])
+            else:
+                nc.scalar.activation(win[t][:], y_ps[t][:], ACT.Exp, scale=0.5)
+        for j, t in enumerate(SCALAR_SLOTS):
+            for c in range(2):
+                nc.scalar.activation(e1[t][:, cols(c)], win[t][:].indirect(piece(n1_t, c)), ACT.Exp, scale=0.5)
+                nc.scalar.activation(e2[j][:, cols(c)], win[t][:].indirect(piece(n2_t, c)), ACT.Exp, scale=0.5)
+        for t in range(PACK):
+            if t not in SCALAR_SLOTS:
+                for c in range(2):
+                    nc.vector.tensor_copy(e1[t][:, cols(c)], win[t][:].indirect(piece(n1_t, c)))
+                for c in range(2):
+                    nc.vector.tensor_tensor(pair[t][:, cols(c)], win[t][:].indirect(piece(n2_t, c)), e1[t][:, cols(c)], ALU.add)
+        for j, t in enumerate(SCALAR_SLOTS):
+            nc.vector.tensor_tensor(pair[t][:], e1[t][:], e2[j][:], ALU.add)
+
+        w2w = deal("w2w", w2w_raw, I32, "e1_1")
+        w2s = deal("w2s", w2s_raw, U8, "e1_2")
+        d_win = [sb(f"d_win{t}", [P, S], F32) for t in range(PACK)]
+        d_own = [sb(f"d_own{t}", [P, S], F32) for t in range(PACK)]
+        for t in range(PACK):
+            nc.scalar.copy(d_win[t][:], d_ps[t][:])
+            nc.sync.dma_start(d_own[t][:], d_win[t][:])
+
+        logs = sb("logs", [P, PACK, S], F32, tag="logs")
+        logit = sb("logit", [P, PACK, S], F32)
+        for t in range(PACK):
+            nc.scalar.activation(logs[:, t, :], pair[t][:], ACT.Ln)
+            nc.vector.scalar_tensor_tensor(logit[:, t, :], y_ps[t][:], 0.5, logs[:, t, :], ALU.mult, ALU.subtract)
+
+        share = [sb(f"share{c}", [P, HALF, PACK], F32) for c in range(2)]
+        z_bf = [sb(f"z_bf{c}", [P, HALF, PACK], BF16, tag=f"z_bf{c}") for c in range(2)]
+        z_w = sb("z_w", [P, S], I32)
+        z_s = sb("z_s", [P, S], U8)
+        h_ps = [psum.tile([P, S], F32, name=f"h_ps{t}", tag=f"hi{t}") for t in range(PACK)]
+        for c in range(2):
+            nc.scalar.activation(
+                share[c][:].rearrange("p (a i) t -> p a t i", i=4),
+                logit[:, :, cols(c)].rearrange("p t (a i) -> p a t i", i=4), ACT.Sigmoid,
+            )
+        for c in range(2):
+            nc.vector.scalar_tensor_tensor(
+                z_bf[c][:], share[c][:], 2.0, gain[:].unsqueeze(1).to_broadcast([P, HALF, PACK]), ALU.mult, ALU.mult,
+            )
+        for c in range(2):
+            nc.vector.quantize_mx(z_w[:, cols(c)].bitcast(FP8X4), z_s[:, cols(c)], z_bf[c][:].rearrange("p s t -> p (s t)"))
+            for t in range(PACK):
+                product(h_ps[t][:, cols(c)], w2w, w2s, t, z_w[:, cols(c)], z_s[:, cols(c)])
+
+        d_first = sb("d_first", [P, PACK - 1, S], F32, tag="logs")
+        d_last = sb("d_last", [P, S], F32, tag="z_bf1")
+        d_sum = [d_first[:, t, :] for t in range(PACK - 1)] + [d_last[:]]
+        gate = sb("gate", [P, PACK, S], F32)
+        for t in range(PACK):
+            for c in range(2):
+                nc.vector.tensor_tensor(d_sum[t][:, cols(c)], d_win[t][:].indirect(piece(n4_t, c)), d_own[t][:, cols(c)], ALU.add)
+            nc.scalar.activation(gate[:, t, :], d_sum[t], ACT.Sigmoid)
+
+        h_win = [sb(f"h_win{t}", [P, S], F32) for t in range(PACK)]
+        h_own = [sb(f"h_own{t}", [P, S], F32) for t in range(PACK)]
+        h_sum = [sb(f"h_sum{t}", [P, S], F32) for t in range(PACK)]
+        o_w = sb("o_w", [P, S], I32)
+        o_s = sb("o_s", [P, S], U8)
+        for t in range(PACK):
+            nc.scalar.copy(h_win[t][:], h_ps[t][:])
+            nc.scalar.copy(h_own[t][:, cols(0)], h_ps[t][:, cols(0)])
+        for t in range(PACK):
+            nc.scalar.copy(h_own[t][:, cols(1)], h_ps[t][:, cols(1)])
+        out_rows = out_0.rearrange("(p t) s -> p t s", t=PACK)
+        out_words = out_1[0].rearrange("p c r -> p (c r)").bitcast(I32)
+        for lo, hi in OUT_PIECES:
+            span = slice(lo, hi)
+            res = sb(f"res{lo}", [P, PACK, hi - lo], F32)
+            res_bf = sb(f"res_bf{lo}", [P, hi - lo, PACK], BF16)
+            for t in range(PACK + 1):
+                if t < PACK:
+                    nc.vector.tensor_tensor(h_sum[t][:, span], h_win[t][:].indirect(n3_t[:, lo // 16 : hi // 16]), h_own[t][:, span], ALU.add)
+                if t > 0:
+                    nc.vector.tensor_tensor(res[:, t - 1, :], h_sum[t - 1][:, span], gate[:, t - 1, span], ALU.mult)
+            nc.sync.dma_start(out_rows[:, :, span], res[:])
+            weave = nc.vector.tensor_copy if hi == S else nc.scalar.copy
+            weave(
+                res_bf[:].rearrange("p (a i) t -> p a t i", i=4),
+                res[:].rearrange("p t (a i) -> p a t i", i=4),
+            )
+            nc.vector.quantize_mx(o_w[:, span].bitcast(FP8X4), o_s[:, span], res_bf[:].rearrange("p s t -> p (s t)"))
+            (nc.scalar if hi == S else nc.sync).dma_start(out_words[:, span], o_w[:, span])
+        for q in range(4):
+            (nc.sync, nc.scalar)[q % 2].dma_start(out_2[0, 4 * q : 4 * q + 4, :].bitcast(I32), o_s[32 * q : 32 * q + 4, :].bitcast(I32))

@@ -19,7 +19,6 @@ P = 128
 PACK = 4
 HALF = S // 2
 SCALAR_SLOTS = (3,)
-OUT_PIECES = ((0, 256), (256, 384), (384, 512))
 
 
 def tile_picked_latetriebshare_none_po_kernel(
@@ -59,33 +58,37 @@ def tile_picked_latetriebshare_none_po_kernel(
 
         def deal(name, raw, dtype, tag=None):
             t = sb(name, [P, PACK, P], dtype, tag)
-            nc.vector.tensor_copy(t[:].rearrange("p t m -> p m t"), raw[:].rearrange("p (m t) -> p m t", t=PACK))
+            if dtype == U8:
+                nc.vector.tensor_copy(t[:], raw[:].rearrange("p (m t) -> p t m", t=PACK))
+            else:
+                nc.vector.tensor_copy(t[:].rearrange("p t m -> p m t"), raw[:].rearrange("p (m t) -> p m t", t=PACK))
             return t
 
         xs_raw = sb("xs_raw", [P, T], U8)
         w1s_raw = sb("w1s_raw", [P, H], U8)
         w3s_raw = sb("w3s_raw", [P, N], U8)
         w2s_raw = sb("w2s_raw", [P, N], U8)
-        nc.vector.memset(xs_raw[:].bitcast(I32), 0)
+        nc.vector.memset(xs_raw[:, : T // 2].bitcast(I32), 0)
+        nc.gpsimd.memset(xs_raw[:, T // 2 :].bitcast(I32), 0)
         for plane in (w1s_raw, w3s_raw, w2s_raw):
             nc.gpsimd.memset(plane[:].bitcast(I32), 0)
 
+        w1w_raw = load_words(nc.scalar, "w1w_raw", w1_words, H)
         offs_t = load_list("offs_t", offs)
         two_t = load_list("two_t", two)
         load_scales(xs_raw, x_scales, (nc.sync, nc.scalar))
-        w1w_raw = load_words(nc.sync, "w1w_raw", w1_words, H)
-        xw_raw = load_words(nc.sync, "xw_raw", x_words, T)
+        xw_raw = load_words(nc.scalar, "xw_raw", x_words, T)
         load_scales(w1s_raw, w1_scales, (nc.sync, nc.sync))
         w3w_raw = load_words(nc.sync, "w3w_raw", w3_words, N)
+        load_scales(w3s_raw, w3_scales, (nc.sync, nc.sync))
         n1_t = load_list("n1_t", n1)
         n2_t = load_list("n2_t", n2)
         n4_t = load_list("n4_t", n4)
         w2w_raw = load_words(nc.sync, "w2w_raw", w2_words, N)
+        load_scales(w2s_raw, w2_scales, (nc.sync, nc.sync))
         n3_t = load_list("n3_t", n3)
-        load_scales(w3s_raw, w3_scales, (nc.gpsimd, nc.gpsimd))
-        load_scales(w2s_raw, w2_scales, (nc.gpsimd, nc.gpsimd))
         gain = sb("gain", [P, PACK], F32)
-        nc.gpsimd.dma_start(gain[:], gn.rearrange("(p t) o -> p (t o)", t=PACK))
+        nc.sync.dma_start(gain[:], gn.rearrange("(p t) o -> p (t o)", t=PACK))
 
         def pick_scales(name, lst):
             t = sb(name, [P, S], U8)
@@ -143,11 +146,11 @@ def tile_picked_latetriebshare_none_po_kernel(
 
         w2w = deal("w2w", w2w_raw, I32, "e1_1")
         w2s = deal("w2s", w2s_raw, U8, "e1_2")
-        d_win = [sb(f"d_win{t}", [P, S], F32) for t in range(PACK)]
-        d_own = [sb(f"d_own{t}", [P, S], F32) for t in range(PACK)]
+        wide = [sb(f"wide{t}", [P, 2 * S], F32) for t in range(PACK)]
+        d_own = [wide[t ^ 1][:, S:] for t in range(PACK)]
         for t in range(PACK):
-            nc.scalar.copy(d_win[t][:], d_ps[t][:])
-            nc.sync.dma_start(d_own[t][:], d_win[t][:])
+            nc.scalar.copy(wide[t][:, :S], d_ps[t][:])
+            nc.sync.dma_start(d_own[t], wide[t][:, :S])
 
         logs = sb("logs", [P, PACK, S], F32, tag="logs")
         logit = sb("logit", [P, PACK, S], F32)
@@ -159,7 +162,7 @@ def tile_picked_latetriebshare_none_po_kernel(
         z_bf = [sb(f"z_bf{c}", [P, HALF, PACK], BF16, tag=f"z_bf{c}") for c in range(2)]
         z_w = sb("z_w", [P, S], I32)
         z_s = sb("z_s", [P, S], U8)
-        h_ps = [psum.tile([P, S], F32, name=f"h_ps{t}", tag=f"hi{t}") for t in range(PACK)]
+        h_ps = [psum.tile([P, S], F32, name=f"h_ps{t}", tag=f"lo{t}") for t in range(PACK)]
         for c in range(2):
             nc.scalar.activation(
                 share[c][:].rearrange("p (a i) t -> p a t i", i=4),
@@ -174,43 +177,67 @@ def tile_picked_latetriebshare_none_po_kernel(
             for t in range(PACK):
                 product(h_ps[t][:, cols(c)], w2w, w2s, t, z_w[:, cols(c)], z_s[:, cols(c)])
 
-        d_first = sb("d_first", [P, PACK - 1, S], F32, tag="logs")
-        d_last = sb("d_last", [P, S], F32, tag="z_bf1")
-        d_sum = [d_first[:, t, :] for t in range(PACK - 1)] + [d_last[:]]
+        d_first = sb("d_first", [P, 2, S], F32, tag="logs")
+        d_sum = [d_first[:, 0, :], d_first[:, 1, :], sb("d_sum2", [P, S], F32, tag="z_bf0")[:], sb("d_sum3", [P, S], F32, tag="z_bf1")[:]]
         gate = sb("gate", [P, PACK, S], F32)
-        for t in range(PACK):
-            for c in range(2):
-                nc.vector.tensor_tensor(d_sum[t][:, cols(c)], d_win[t][:].indirect(piece(n4_t, c)), d_own[t][:, cols(c)], ALU.add)
-            nc.scalar.activation(gate[:, t, :], d_sum[t], ACT.Sigmoid)
-
-        h_win = [sb(f"h_win{t}", [P, S], F32) for t in range(PACK)]
-        h_own = [sb(f"h_own{t}", [P, S], F32) for t in range(PACK)]
-        h_sum = [sb(f"h_sum{t}", [P, S], F32) for t in range(PACK)]
+        h_own = sb("h_own", [P, PACK, S], F32)
+        h_sum = sb("h_sum", [P, PACK, S], F32)
+        res = sb("res", [P, PACK, S], F32)
         o_w = sb("o_w", [P, S], I32)
         o_s = sb("o_s", [P, S], U8)
-        for t in range(PACK):
-            nc.scalar.copy(h_win[t][:], h_ps[t][:])
-            nc.scalar.copy(h_own[t][:, cols(0)], h_ps[t][:, cols(0)])
-        for t in range(PACK):
-            nc.scalar.copy(h_own[t][:, cols(1)], h_ps[t][:, cols(1)])
         out_rows = out_0.rearrange("(p t) s -> p t s", t=PACK)
         out_words = out_1[0].rearrange("p c r -> p (c r)").bitcast(I32)
-        for lo, hi in OUT_PIECES:
-            span = slice(lo, hi)
-            res = sb(f"res{lo}", [P, PACK, hi - lo], F32)
-            res_bf = sb(f"res_bf{lo}", [P, hi - lo, PACK], BF16)
-            for t in range(PACK + 1):
-                if t < PACK:
-                    nc.vector.tensor_tensor(h_sum[t][:, span], h_win[t][:].indirect(n3_t[:, lo // 16 : hi // 16]), h_own[t][:, span], ALU.add)
-                if t > 0:
-                    nc.vector.tensor_tensor(res[:, t - 1, :], h_sum[t - 1][:, span], gate[:, t - 1, span], ALU.mult)
-            nc.sync.dma_start(out_rows[:, :, span], res[:])
-            weave = nc.vector.tensor_copy if hi == S else nc.scalar.copy
-            weave(
-                res_bf[:].rearrange("p (a i) t -> p a t i", i=4),
-                res[:].rearrange("p t (a i) -> p a t i", i=4),
-            )
-            nc.vector.quantize_mx(o_w[:, span].bitcast(FP8X4), o_s[:, span], res_bf[:].rearrange("p s t -> p (s t)"))
-            (nc.scalar if hi == S else nc.sync).dma_start(out_words[:, span], o_w[:, span])
+
+        def gather_d(t):
+            nc.vector.tensor_tensor(d_sum[t], wide[t][:].indirect(n4_t[:]), d_own[t], ALU.add)
+
+        def make_gate(t):
+            nc.scalar.activation(gate[:, t, :], d_sum[t], ACT.Sigmoid)
+
+        def copy_h(t):
+            nc.scalar.copy(wide[t][:, :S], h_ps[t][:])
+            nc.scalar.copy(h_own[:, t, :], h_ps[t][:])
+
+        def gather_h(t, span):
+            nc.vector.tensor_tensor(
+                h_sum[:, t, span], wide[t][:].indirect(n3_t[:, span.start // 16 : span.stop // 16]), h_own[:, t, span], ALU.add)
+
+        def finish(slots, span):
+            nc.vector.tensor_tensor(res[:, slots, span], h_sum[:, slots, span], gate[:, slots, span], ALU.mult)
+            nc.sync.dma_start(out_rows[:, slots, span], res[:, slots, span])
+
+        def weave(engine_copy, c):
+            woven = sb(f"res_bf{c}", [P, HALF, PACK], BF16)
+            engine_copy(woven[:].rearrange("p (a i) t -> p a t i", i=4), res[:, :, cols(c)].rearrange("p t (a i) -> p a t i", i=4))
+            return woven
+
+        def quantise(woven, c, queue):
+            nc.vector.quantize_mx(o_w[:, cols(c)].bitcast(FP8X4), o_s[:, cols(c)], woven[:].rearrange("p s t -> p (s t)"))
+            queue.dma_start(out_words[:, cols(c)], o_w[:, cols(c)])
+
+        for t in range(PACK):
+            gather_d(t)
+        make_gate(0)
+        make_gate(1)
+        copy_h(0)
+        copy_h(1)
+        make_gate(2)
+        copy_h(2)
+        make_gate(3)
+        copy_h(3)
+        whole = slice(0, S)
+        gather_h(0, whole)
+        gather_h(1, whole)
+        finish(slice(0, 1), whole)
+        gather_h(2, cols(0))
+        finish(slice(1, 2), whole)
+        gather_h(3, cols(0))
+        gather_h(2, cols(1))
+        finish(slice(2, 4), cols(0))
+        first = weave(nc.scalar.copy, 0)
+        gather_h(3, cols(1))
+        finish(slice(2, 4), cols(1))
+        quantise(first, 0, nc.sync)
+        quantise(weave(nc.vector.tensor_copy, 1), 1, nc.scalar)
         for q in range(4):
             (nc.sync, nc.scalar)[q % 2].dma_start(out_2[0, 4 * q : 4 * q + 4, :].bitcast(I32), o_s[32 * q : 32 * q + 4, :].bitcast(I32))

@@ -43,10 +43,10 @@ def tile_picked_latetriebshare_none_po_kernel(
             queue.dma_start(t[:], src[0].rearrange("p c r -> p (c r)").bitcast(I32))
             return t
 
-        def load_scales(plane, src, queues):
+        def load_scales(plane, first, src, queues):
             for q in range(4):
                 queues[q % 2].dma_start(
-                    plane[32 * q : 32 * q + 4, :].bitcast(I32),
+                    plane[32 * q + first : 32 * q + first + 4, :].bitcast(I32),
                     src[0, 4 * q : 4 * q + 4, :].bitcast(I32),
                 )
 
@@ -61,31 +61,30 @@ def tile_picked_latetriebshare_none_po_kernel(
             if dtype == U8:
                 nc.vector.tensor_copy(t[:], raw[:].rearrange("p (m t) -> p t m", t=PACK))
             else:
-                nc.vector.tensor_copy(t[:].rearrange("p t m -> p m t"), raw[:].rearrange("p (m t) -> p m t", t=PACK))
+                nc.vector.tensor_copy(t[:].rearrange("p t (a i) -> p a t i", i=4), raw[:].rearrange("p (a i t) -> p a t i", i=4, t=PACK))
             return t
 
         xs_raw = sb("xs_raw", [P, T], U8)
         w1s_raw = sb("w1s_raw", [P, H], U8)
-        w3s_raw = sb("w3s_raw", [P, N], U8)
-        w2s_raw = sb("w2s_raw", [P, N], U8)
+        w32s_raw = sb("w32s_raw", [P, N], U8)
         nc.vector.memset(xs_raw[:, : T // 2].bitcast(I32), 0)
         nc.gpsimd.memset(xs_raw[:, T // 2 :].bitcast(I32), 0)
-        for plane in (w1s_raw, w3s_raw, w2s_raw):
+        for plane in (w1s_raw, w32s_raw):
             nc.gpsimd.memset(plane[:].bitcast(I32), 0)
 
         w1w_raw = load_words(nc.scalar, "w1w_raw", w1_words, H)
         offs_t = load_list("offs_t", offs)
         two_t = load_list("two_t", two)
-        load_scales(xs_raw, x_scales, (nc.sync, nc.scalar))
+        load_scales(xs_raw, 0, x_scales, (nc.sync, nc.scalar))
         xw_raw = load_words(nc.scalar, "xw_raw", x_words, T)
-        load_scales(w1s_raw, w1_scales, (nc.sync, nc.sync))
+        load_scales(w1s_raw, 0, w1_scales, (nc.sync, nc.sync))
         w3w_raw = load_words(nc.sync, "w3w_raw", w3_words, N)
-        load_scales(w3s_raw, w3_scales, (nc.sync, nc.sync))
+        load_scales(w32s_raw, 0, w3_scales, (nc.sync, nc.sync))
+        load_scales(w32s_raw, 4, w2_scales, (nc.sync, nc.sync))
         n1_t = load_list("n1_t", n1)
         n2_t = load_list("n2_t", n2)
         n4_t = load_list("n4_t", n4)
         w2w_raw = load_words(nc.sync, "w2w_raw", w2_words, N)
-        load_scales(w2s_raw, w2_scales, (nc.sync, nc.sync))
         n3_t = load_list("n3_t", n3)
         gain = sb("gain", [P, PACK], F32)
         nc.sync.dma_start(gain[:], gn.rearrange("(p t) o -> p (t o)", t=PACK))
@@ -107,20 +106,20 @@ def tile_picked_latetriebshare_none_po_kernel(
         w1s = deal("w1s", w1s_raw, U8)
         xb_w = pick_words("xb_w", two_t, "w1s_raw")
         w3w = deal("w3w", w3w_raw, I32)
-        w3s = deal("w3s", w3s_raw, U8, "w3w_raw")
+        w32s = deal("w32s", w32s_raw, U8)
 
-        def product(bank, ww, ws, t, xw, xs):
+        def product(bank, ww, ws, first, t, xw, xs):
             nc.tensor.matmul_mx(
-                out=bank, lhsT=ww[:, t, :].bitcast(FP8X4), lhsT_scale=ws[:, t, :],
+                out=bank, lhsT=ww[:, t, :].bitcast(FP8X4), lhsT_scale=ws[first:P, t, :],
                 rhs=xw.bitcast(FP8X4), rhs_scale=xs, start=True, stop=True,
             )
 
         y_ps = [psum.tile([P, S], F32, name=f"y_ps{t}", tag=f"lo{t}") for t in range(PACK)]
         d_ps = [psum.tile([P, S], F32, name=f"d_ps{t}", tag=f"hi{t}") for t in range(PACK)]
         for t in range(PACK):
-            product(y_ps[t][:], w1w, w1s, t, xa_w[:], xa_s[:])
+            product(y_ps[t][:], w1w, w1s, 0, t, xa_w[:], xa_s[:])
         for t in range(PACK):
-            product(d_ps[t][:], w3w, w3s, t, xb_w[:], xb_s[:])
+            product(d_ps[t][:], w3w, w32s, 0, t, xb_w[:], xb_s[:])
 
         win = [sb(f"win{t}", [P, S], F32) for t in range(PACK)]
         e1 = [sb(f"e1_{t}", [P, S], F32) for t in range(PACK)]
@@ -145,7 +144,6 @@ def tile_picked_latetriebshare_none_po_kernel(
             nc.vector.tensor_tensor(pair[t][:], e1[t][:], e2[j][:], ALU.add)
 
         w2w = deal("w2w", w2w_raw, I32, "e1_1")
-        w2s = deal("w2s", w2s_raw, U8, "e1_2")
         wide = [sb(f"wide{t}", [P, 2 * S], F32) for t in range(PACK)]
         d_own = [wide[t ^ 1][:, S:] for t in range(PACK)]
         for t in range(PACK):
@@ -165,8 +163,8 @@ def tile_picked_latetriebshare_none_po_kernel(
         h_ps = [psum.tile([P, S], F32, name=f"h_ps{t}", tag=f"lo{t}") for t in range(PACK)]
         for c in range(2):
             nc.scalar.activation(
-                share[c][:].rearrange("p (a i) t -> p a t i", i=4),
-                logit[:, :, cols(c)].rearrange("p t (a i) -> p a t i", i=4), ACT.Sigmoid,
+                share[c][:].rearrange("p (a i) t -> p a t i", i=2),
+                logit[:, :, cols(c)].rearrange("p t (a i) -> p a t i", i=2), ACT.Sigmoid,
             )
         for c in range(2):
             nc.vector.scalar_tensor_tensor(
@@ -175,7 +173,7 @@ def tile_picked_latetriebshare_none_po_kernel(
         for c in range(2):
             nc.vector.quantize_mx(z_w[:, cols(c)].bitcast(FP8X4), z_s[:, cols(c)], z_bf[c][:].rearrange("p s t -> p (s t)"))
             for t in range(PACK):
-                product(h_ps[t][:, cols(c)], w2w, w2s, t, z_w[:, cols(c)], z_s[:, cols(c)])
+                product(h_ps[t][:, cols(c)], w2w, w32s, 4, t, z_w[:, cols(c)], z_s[:, cols(c)])
 
         d_first = sb("d_first", [P, 2, S], F32, tag="logs")
         d_sum = [d_first[:, 0, :], d_first[:, 1, :], sb("d_sum2", [P, S], F32, tag="z_bf0")[:], sb("d_sum3", [P, S], F32, tag="z_bf1")[:]]

@@ -1,6 +1,7 @@
 from contextlib import ExitStack
 
 import concourse.mybir as mybir
+from concourse.masks import make_identity
 
 K, T, S, N, H = 512, 2048, 512, 512, 512
 FLOPS = 3 * 2 * 512 * 512 * 512
@@ -18,7 +19,6 @@ ALU = mybir.AluOpType
 P = 128
 PACK = 4
 HALF = S // 2
-SCALAR_SLOTS = (3,)
 
 
 def tile_picked_latetriebshare_none_po_kernel(
@@ -72,6 +72,9 @@ def tile_picked_latetriebshare_none_po_kernel(
         for plane in (w1s_raw, w32s_raw):
             nc.gpsimd.memset(plane[:].bitcast(I32), 0)
 
+        ident = sb("ident", [P, P], F32)
+        make_identity(nc, ident[:])
+
         w1w_raw = load_words(nc.scalar, "w1w_raw", w1_words, H)
         offs_t = load_list("offs_t", offs)
         two_t = load_list("two_t", two)
@@ -94,17 +97,17 @@ def tile_picked_latetriebshare_none_po_kernel(
             nc.vector.tensor_copy(t[:], xs_raw[:].indirect(lst[:]))
             return t
 
-        def pick_words(name, lst, tag=None):
-            t = sb(name, [P, S], I32, tag)
-            nc.vector.tensor_copy(t[:].bitcast(U32), xw_raw[:].bitcast(U32).indirect(lst[:]))
-            return t
+        def pick_words(dst, offsets):
+            nc.vector.tensor_copy(dst.bitcast(U32), xw_raw[:].bitcast(U32).indirect(offsets))
 
         xa_s = pick_scales("xa_s", offs_t)
         w1w = deal("w1w", w1w_raw, I32)
         xb_s = pick_scales("xb_s", two_t)
-        xa_w = pick_words("xa_w", offs_t)
+        xa_w = sb("xa_w", [P, S], I32)
+        xb_w = sb("xb_w", [P, S], I32, "w1s_raw")
+        pick_words(xa_w[:], offs_t[:])
         w1s = deal("w1s", w1s_raw, U8)
-        xb_w = pick_words("xb_w", two_t, "w1s_raw")
+        pick_words(xb_w[:], two_t[:])
         w3w = deal("w3w", w3w_raw, I32)
         w32s = deal("w32s", w32s_raw, U8)
 
@@ -121,39 +124,51 @@ def tile_picked_latetriebshare_none_po_kernel(
         for t in range(PACK):
             product(d_ps[t][:], w3w, w32s, 0, t, xb_w[:], xb_s[:])
 
-        win = [sb(f"win{t}", [P, S], F32) for t in range(PACK)]
-        e1 = [sb(f"e1_{t}", [P, S], F32) for t in range(PACK)]
-        e2 = [sb(f"e2_{t}", [P, S], F32) for t in SCALAR_SLOTS]
-        pair = [sb(f"pair{t}", [P, S], F32) for t in range(PACK)]
-        for t in range(PACK):
-            if t in SCALAR_SLOTS:
-                nc.scalar.copy(win[t][:], y_ps[t][:])
-            else:
-                nc.scalar.activation(win[t][:], y_ps[t][:], ACT.Exp, scale=0.5)
-        for j, t in enumerate(SCALAR_SLOTS):
+        ex0 = sb("ex0", [P, S], F32)
+        ex1 = sb("ex1", [P, 2 * S], F32)
+        ex2 = sb("ex2", [P, 2 * S], F32)
+        y3 = sb("y3", [P, S], F32)
+        e1 = [ex1[:, S:]] + [sb(f"e1_{t}", [P, S], F32)[:] for t in range(1, PACK)]
+        e2_last = sb("e2_last", [P, S], F32)
+        pair = [ex2[:, S:]] + [sb(f"pair{t}", [P, S], F32)[:] for t in range(1, 3)]
+        for t, win in enumerate((ex0, ex1, ex2)):
+            nc.scalar.activation(win[:, :S], y_ps[t][:], ACT.Exp, scale=0.5)
+        nc.scalar.copy(y3[:], y_ps[3][:])
+        for dst, lst in ((e1[3], n1_t), (e2_last[:], n2_t)):
             for c in range(2):
-                nc.scalar.activation(e1[t][:, cols(c)], win[t][:].indirect(piece(n1_t, c)), ACT.Exp, scale=0.5)
-                nc.scalar.activation(e2[j][:, cols(c)], win[t][:].indirect(piece(n2_t, c)), ACT.Exp, scale=0.5)
-        for t in range(PACK):
-            if t not in SCALAR_SLOTS:
-                for c in range(2):
-                    nc.vector.tensor_copy(e1[t][:, cols(c)], win[t][:].indirect(piece(n1_t, c)))
-                for c in range(2):
-                    nc.vector.tensor_tensor(pair[t][:, cols(c)], win[t][:].indirect(piece(n2_t, c)), e1[t][:, cols(c)], ALU.add)
-        for j, t in enumerate(SCALAR_SLOTS):
-            nc.vector.tensor_tensor(pair[t][:], e1[t][:], e2[j][:], ALU.add)
+                nc.scalar.activation(dst[:, cols(c)], y3[:].indirect(piece(lst, c)), ACT.Exp, scale=0.5)
+        for c in range(2):
+            nc.vector.tensor_copy(e1[0][:, cols(c)], ex0[:].indirect(piece(n1_t, c)))
+        for c in range(2):
+            nc.vector.tensor_tensor(pair[0][:, cols(c)], ex0[:].indirect(piece(n2_t, c)), e1[0][:, cols(c)], ALU.add)
+        for t, win in ((1, ex1), (2, ex2)):
+            nc.vector.tensor_copy(e1[t], win[:].indirect(n1_t[:]))
+        for t, win in ((1, ex1), (2, ex2)):
+            nc.vector.tensor_tensor(pair[t], win[:].indirect(n2_t[:]), e1[t], ALU.add)
+        pair3_ps = psum.tile([P, S], F32, name="pair3_ps", tag="lo3")
+        for b in range(S // P):
+            blk = slice(b * P, (b + 1) * P)
+            nc.tensor.matmul(pair3_ps[:, blk], e1[3][:, blk], ident[:], start=True, stop=False, is_transpose=True)
+            nc.tensor.matmul(pair3_ps[:, blk], e2_last[:, blk], ident[:], start=False, stop=True, is_transpose=True)
 
         w2w = deal("w2w", w2w_raw, I32, "e1_1")
-        wide = [sb(f"wide{t}", [P, 2 * S], F32) for t in range(PACK)]
-        d_own = [wide[t ^ 1][:, S:] for t in range(PACK)]
-        for t in range(PACK):
+        wide = [sb(f"wide{t}", [P, 2 * S], F32) for t in (0, 1)]
+        d_own = [wide[1][:, S:], wide[0][:, S:]]
+        for t in (0, 1):
             nc.scalar.copy(wide[t][:, :S], d_ps[t][:])
             nc.sync.dma_start(d_own[t], wide[t][:, :S])
 
-        logs = sb("logs", [P, PACK, S], F32, tag="logs")
+        logs = sb("logs", [P, 3, S], F32, tag="logs")
         logit = sb("logit", [P, PACK, S], F32)
-        for t in range(PACK):
-            nc.scalar.activation(logs[:, t, :], pair[t][:], ACT.Ln)
+        log3_turned = sb("log3_turned", [P, S], F32)
+        nc.scalar.activation(log3_turned[:], pair3_ps[:], ACT.Ln)
+        log3_ps = psum.tile([P, S], F32, name="log3_ps", tag="lo3")
+        for b in range(S // P):
+            blk = slice(b * P, (b + 1) * P)
+            nc.tensor.transpose(log3_ps[:, blk], log3_turned[:, blk], ident[:])
+        nc.vector.scalar_tensor_tensor(logit[:, 3, :], y3[:], 0.5, log3_ps[:], ALU.mult, ALU.subtract)
+        for t in range(3):
+            nc.scalar.activation(logs[:, t, :], pair[t], ACT.Ln)
             nc.vector.scalar_tensor_tensor(logit[:, t, :], y_ps[t][:], 0.5, logs[:, t, :], ALU.mult, ALU.subtract)
 
         share = [sb(f"share{c}", [P, HALF, PACK], F32) for c in range(2)]
@@ -175,6 +190,11 @@ def tile_picked_latetriebshare_none_po_kernel(
             for t in range(PACK):
                 product(h_ps[t][:, cols(c)], w2w, w32s, 4, t, z_w[:, cols(c)], z_s[:, cols(c)])
 
+        wide.extend([sb("wide2", [P, 2 * S], F32, "logit"), sb("wide3", [P, 2 * S], F32, "share0")])
+        d_own.extend([wide[3][:, S:], wide[2][:, S:]])
+        for t in (2, 3):
+            nc.scalar.copy(wide[t][:, :S], d_ps[t][:])
+            nc.scalar.copy(d_own[t], d_ps[t][:])
         d_first = sb("d_first", [P, 2, S], F32, tag="logs")
         d_sum = [d_first[:, 0, :], d_first[:, 1, :], sb("d_sum2", [P, S], F32, tag="z_bf0")[:], sb("d_sum3", [P, S], F32, tag="z_bf1")[:]]
         gate = sb("gate", [P, PACK, S], F32)

@@ -4,7 +4,7 @@ import concourse.mybir as mybir
 from concourse.masks import make_identity
 
 K, T, S, N, H = 512, 2048, 512, 512, 512
-FLOPS = 3 * 2 * 512 * 512 * 512
+FLOPS = 2 * K * H * S + 2 * H * N * S + 2 * K * N * S
 
 F32 = mybir.dt.float32
 BF16 = mybir.dt.bfloat16
@@ -17,8 +17,11 @@ ACT = mybir.ActivationFunctionType
 ALU = mybir.AluOpType
 
 P = 128
-PACK = 4
+SLOTS = 4
 HALF = S // 2
+GROUP = 16
+QUADRANT = 32
+W3_ROW, W2_ROW = 0, 4
 
 
 def tile_picked_latetriebshare_none_po_kernel(
@@ -30,47 +33,50 @@ def tile_picked_latetriebshare_none_po_kernel(
         keep = ctx.enter_context(tc.tile_pool(name="keep", bufs=1))
         psum = ctx.enter_context(tc.psum_pool(name="psum", bufs=1))
 
-        def sb(name, shape, dtype, tag=None):
-            return keep.tile(shape, dtype, name=name, tag=tag or name, align_bytes=64)
+        halves = (slice(0, HALF), slice(HALF, S))
+        whole = slice(0, S)
+        blocks = [slice(b * P, (b + 1) * P) for b in range(S // P)]
+
+        def sb(name, shape, dtype, reuses=None):
+            return keep.tile(shape, dtype, name=name, tag=reuses or name, align_bytes=64)
+
+        def entries(lst, span):
+            return lst[:, span.start // GROUP : span.stop // GROUP]
 
         def load_list(name, src):
-            t = sb(name, [P, S // 16], U16)
-            nc.sync.dma_start(t[:], src)
-            return t
+            tile = sb(name, [P, S // GROUP], U16)
+            nc.sync.dma_start(tile[:], src)
+            return tile
 
         def load_words(queue, name, src, width):
-            t = sb(name, [P, width], I32)
-            queue.dma_start(t[:], src[0].rearrange("p c r -> p (c r)").bitcast(I32))
-            return t
+            tile = sb(name, [P, width], I32)
+            queue.dma_start(tile[:], src[0].rearrange("p c r -> p (c r)").bitcast(I32))
+            return tile
 
-        def load_scales(plane, first, src, queues):
-            for q in range(4):
-                queues[q % 2].dma_start(
-                    plane[32 * q + first : 32 * q + first + 4, :].bitcast(I32),
-                    src[0, 4 * q : 4 * q + 4, :].bitcast(I32),
-                )
+        def load_scales(tile, first_row, src, queues):
+            for q in range(P // QUADRANT):
+                row = QUADRANT * q + first_row
+                queues[q % 2].dma_start(tile[row : row + 4, :].bitcast(I32), src[0, 4 * q : 4 * q + 4, :].bitcast(I32))
 
-        def piece(lst, c):
-            return lst[:, c * (HALF // 16) : (c + 1) * (HALF // 16)]
+        def deal_words(name, raw, reuses=None):
+            tile = sb(name, [P, SLOTS, P], I32, reuses)
+            nc.vector.tensor_copy(
+                tile[:].rearrange("p t (a i) -> p a t i", i=4), raw[:].rearrange("p (a i t) -> p a t i", i=4, t=SLOTS)
+            )
+            return tile
 
-        def cols(c):
-            return slice(c * HALF, (c + 1) * HALF)
-
-        def deal(name, raw, dtype, tag=None):
-            t = sb(name, [P, PACK, P], dtype, tag)
-            if dtype == U8:
-                nc.vector.tensor_copy(t[:], raw[:].rearrange("p (m t) -> p t m", t=PACK))
-            else:
-                nc.vector.tensor_copy(t[:].rearrange("p t (a i) -> p a t i", i=4), raw[:].rearrange("p (a i t) -> p a t i", i=4, t=PACK))
-            return t
+        def deal_scales(name, raw):
+            tile = sb(name, [P, SLOTS, P], U8)
+            nc.vector.tensor_copy(tile[:], raw[:].rearrange("p (m t) -> p t m", t=SLOTS))
+            return tile
 
         xs_raw = sb("xs_raw", [P, T], U8)
         w1s_raw = sb("w1s_raw", [P, H], U8)
         w32s_raw = sb("w32s_raw", [P, N], U8)
         nc.vector.memset(xs_raw[:, : T // 2].bitcast(I32), 0)
         nc.gpsimd.memset(xs_raw[:, T // 2 :].bitcast(I32), 0)
-        for plane in (w1s_raw, w32s_raw):
-            nc.gpsimd.memset(plane[:].bitcast(I32), 0)
+        for tile in (w1s_raw, w32s_raw):
+            nc.gpsimd.memset(tile[:].bitcast(I32), 0)
 
         ident = sb("ident", [P, P], F32)
         make_identity(nc, ident[:])
@@ -82,180 +88,199 @@ def tile_picked_latetriebshare_none_po_kernel(
         xw_raw = load_words(nc.scalar, "xw_raw", x_words, T)
         load_scales(w1s_raw, 0, w1_scales, (nc.sync, nc.sync))
         w3w_raw = load_words(nc.sync, "w3w_raw", w3_words, N)
-        load_scales(w32s_raw, 0, w3_scales, (nc.sync, nc.sync))
-        load_scales(w32s_raw, 4, w2_scales, (nc.sync, nc.sync))
+        load_scales(w32s_raw, W3_ROW, w3_scales, (nc.sync, nc.sync))
+        load_scales(w32s_raw, W2_ROW, w2_scales, (nc.sync, nc.sync))
         n1_t = load_list("n1_t", n1)
         n2_t = load_list("n2_t", n2)
         n4_t = load_list("n4_t", n4)
         w2w_raw = load_words(nc.sync, "w2w_raw", w2_words, N)
         n3_t = load_list("n3_t", n3)
-        gain = sb("gain", [P, PACK], F32)
-        nc.sync.dma_start(gain[:], gn.rearrange("(p t) o -> p (t o)", t=PACK))
+        gain = sb("gain", [P, SLOTS], F32)
+        nc.sync.dma_start(gain[:], gn.rearrange("(p t) o -> p (t o)", t=SLOTS))
 
         def pick_scales(name, lst):
-            t = sb(name, [P, S], U8)
-            nc.vector.tensor_copy(t[:], xs_raw[:].indirect(lst[:]))
-            return t
+            tile = sb(name, [P, S], U8)
+            nc.vector.tensor_copy(tile[:], xs_raw[:].indirect(lst[:]))
+            return tile
 
-        def pick_words(dst, offsets):
-            nc.vector.tensor_copy(dst.bitcast(U32), xw_raw[:].bitcast(U32).indirect(offsets))
+        def pick_words(tile, lst):
+            nc.vector.tensor_copy(tile[:].bitcast(U32), xw_raw[:].bitcast(U32).indirect(lst[:]))
 
         xa_s = pick_scales("xa_s", offs_t)
-        w1w = deal("w1w", w1w_raw, I32)
+        w1w = deal_words("w1w", w1w_raw)
         xb_s = pick_scales("xb_s", two_t)
         xa_w = sb("xa_w", [P, S], I32)
-        xb_w = sb("xb_w", [P, S], I32, "w1s_raw")
-        pick_words(xa_w[:], offs_t[:])
-        w1s = deal("w1s", w1s_raw, U8)
-        pick_words(xb_w[:], two_t[:])
-        w3w = deal("w3w", w3w_raw, I32)
-        w32s = deal("w32s", w32s_raw, U8)
+        xb_w = sb("xb_w", [P, S], I32, reuses="w1s_raw")
+        pick_words(xa_w, offs_t)
+        w1s = deal_scales("w1s", w1s_raw)
+        pick_words(xb_w, two_t)
+        w3w = deal_words("w3w", w3w_raw)
+        w32s = deal_scales("w32s", w32s_raw)
 
-        def product(bank, ww, ws, first, t, xw, xs):
+        def product(out, w_words, w_scales, first_row, t, words, scales):
             nc.tensor.matmul_mx(
-                out=bank, lhsT=ww[:, t, :].bitcast(FP8X4), lhsT_scale=ws[first:P, t, :],
-                rhs=xw.bitcast(FP8X4), rhs_scale=xs, start=True, stop=True,
+                out=out, lhsT=w_words[:, t, :].bitcast(FP8X4), lhsT_scale=w_scales[first_row:P, t, :],
+                rhs=words.bitcast(FP8X4), rhs_scale=scales, start=True, stop=True,
             )
 
-        y_ps = [psum.tile([P, S], F32, name=f"y_ps{t}", tag=f"lo{t}") for t in range(PACK)]
-        d_ps = [psum.tile([P, S], F32, name=f"d_ps{t}", tag=f"hi{t}") for t in range(PACK)]
-        for t in range(PACK):
+        y_ps = [psum.tile([P, S], F32, name=f"y_ps{t}", tag=f"lo{t}") for t in range(SLOTS)]
+        d_ps = [psum.tile([P, S], F32, name=f"d_ps{t}", tag=f"hi{t}") for t in range(SLOTS)]
+        for t in range(SLOTS):
             product(y_ps[t][:], w1w, w1s, 0, t, xa_w[:], xa_s[:])
-        for t in range(PACK):
-            product(d_ps[t][:], w3w, w32s, 0, t, xb_w[:], xb_s[:])
+        for t in range(SLOTS):
+            product(d_ps[t][:], w3w, w32s, W3_ROW, t, xb_w[:], xb_s[:])
 
         ex0 = sb("ex0", [P, S], F32)
         ex1 = sb("ex1", [P, 2 * S], F32)
         ex2 = sb("ex2", [P, 2 * S], F32)
         y3 = sb("y3", [P, S], F32)
-        e1 = [ex1[:, S:]] + [sb(f"e1_{t}", [P, S], F32)[:] for t in range(1, PACK)]
-        e2_last = sb("e2_last", [P, S], F32)
-        pair = [ex2[:, S:]] + [sb(f"pair{t}", [P, S], F32)[:] for t in range(1, 3)]
+        dh_win = [sb(f"dh_win{t}", [P, 2 * S], F32) for t in (0, 1)]
+        near = [ex1[:, S:], dh_win[0][:, S:], dh_win[1][:, S:], sb("near3", [P, S], F32)[:]]
+        far3 = sb("far3", [P, S], F32)
+        pair = [ex2[:, S:]] + [sb(f"pair{t}", [P, S], F32)[:] for t in (1, 2)]
         for t, win in enumerate((ex0, ex1, ex2)):
             nc.scalar.activation(win[:, :S], y_ps[t][:], ACT.Exp, scale=0.5)
         nc.scalar.copy(y3[:], y_ps[3][:])
-        for dst, lst in ((e1[3], n1_t), (e2_last[:], n2_t)):
-            for c in range(2):
-                nc.scalar.activation(dst[:, cols(c)], y3[:].indirect(piece(lst, c)), ACT.Exp, scale=0.5)
-        for c in range(2):
-            nc.vector.tensor_copy(e1[0][:, cols(c)], ex0[:].indirect(piece(n1_t, c)))
-        for c in range(2):
-            nc.vector.tensor_tensor(pair[0][:, cols(c)], ex0[:].indirect(piece(n2_t, c)), e1[0][:, cols(c)], ALU.add)
+        for dst, lst in ((near[3], n1_t), (far3[:], n2_t)):
+            for span in halves:
+                nc.scalar.activation(dst[:, span], y3[:].indirect(entries(lst, span)), ACT.Exp, scale=0.5)
+        for span in halves:
+            nc.vector.tensor_copy(near[0][:, span], ex0[:].indirect(entries(n1_t, span)))
+        for span in halves:
+            nc.vector.tensor_tensor(pair[0][:, span], ex0[:].indirect(entries(n2_t, span)), near[0][:, span], ALU.add)
         for t, win in ((1, ex1), (2, ex2)):
-            nc.vector.tensor_copy(e1[t], win[:].indirect(n1_t[:]))
+            nc.vector.tensor_copy(near[t], win[:].indirect(n1_t[:]))
         for t, win in ((1, ex1), (2, ex2)):
-            nc.vector.tensor_tensor(pair[t], win[:].indirect(n2_t[:]), e1[t], ALU.add)
-        pair3_ps = psum.tile([P, S], F32, name="pair3_ps", tag="lo3")
-        for b in range(S // P):
-            blk = slice(b * P, (b + 1) * P)
-            nc.tensor.matmul(pair3_ps[:, blk], e1[3][:, blk], ident[:], start=True, stop=False, is_transpose=True)
-            nc.tensor.matmul(pair3_ps[:, blk], e2_last[:, blk], ident[:], start=False, stop=True, is_transpose=True)
+            nc.vector.tensor_tensor(pair[t], win[:].indirect(n2_t[:]), near[t], ALU.add)
 
-        w2w = deal("w2w", w2w_raw, I32, "e1_1")
-        wide = [sb(f"wide{t}", [P, 2 * S], F32) for t in (0, 1)]
-        d_own = [wide[1][:, S:], wide[0][:, S:]]
+        def turned_sum(name, bank, first, second):
+            acc = psum.tile([P, S], F32, name=name, tag=bank)
+            for blk in blocks:
+                nc.tensor.matmul(acc[:, blk], first[:, blk], ident[:], start=True, stop=False, is_transpose=True)
+                nc.tensor.matmul(acc[:, blk], second[:, blk], ident[:], start=False, stop=True, is_transpose=True)
+            return acc
+
+        pair3_ps = turned_sum("pair3_ps", "lo3", near[3], far3[:])
+
+        w2w = deal_words("w2w", w2w_raw, reuses="ex1")
         for t in (0, 1):
-            nc.scalar.copy(wide[t][:, :S], d_ps[t][:])
-            nc.sync.dma_start(d_own[t], wide[t][:, :S])
+            nc.scalar.copy(dh_win[t][:, :S], d_ps[t][:])
 
-        logs = sb("logs", [P, 3, S], F32, tag="logs")
-        logit = sb("logit", [P, PACK, S], F32)
+        logs = sb("logs", [P, 3, S], F32)
+        logit = sb("logit", [P, SLOTS, S], F32)
         log3_turned = sb("log3_turned", [P, S], F32)
         nc.scalar.activation(log3_turned[:], pair3_ps[:], ACT.Ln)
         log3_ps = psum.tile([P, S], F32, name="log3_ps", tag="lo3")
-        for b in range(S // P):
-            blk = slice(b * P, (b + 1) * P)
+        for blk in blocks:
             nc.tensor.transpose(log3_ps[:, blk], log3_turned[:, blk], ident[:])
         nc.vector.scalar_tensor_tensor(logit[:, 3, :], y3[:], 0.5, log3_ps[:], ALU.mult, ALU.subtract)
         for t in range(3):
             nc.scalar.activation(logs[:, t, :], pair[t], ACT.Ln)
             nc.vector.scalar_tensor_tensor(logit[:, t, :], y_ps[t][:], 0.5, logs[:, t, :], ALU.mult, ALU.subtract)
 
-        share = [sb(f"share{c}", [P, HALF, PACK], F32) for c in range(2)]
-        z_bf = [sb(f"z_bf{c}", [P, HALF, PACK], BF16, tag=f"z_bf{c}") for c in range(2)]
+        share = [sb(f"share{c}", [P, HALF, SLOTS], F32) for c in range(2)]
+        z_bf = [sb(f"z_bf{c}", [P, HALF, SLOTS], BF16) for c in range(2)]
         z_w = sb("z_w", [P, S], I32)
         z_s = sb("z_s", [P, S], U8)
-        h_ps = [psum.tile([P, S], F32, name=f"h_ps{t}", tag=f"lo{t}") for t in range(PACK)]
-        for c in range(2):
+        h_ps = [psum.tile([P, S], F32, name=f"h_ps{t}", tag=f"lo{t}") for t in range(SLOTS)]
+        for c, span in enumerate(halves):
             nc.scalar.activation(
                 share[c][:].rearrange("p (a i) t -> p a t i", i=2),
-                logit[:, :, cols(c)].rearrange("p t (a i) -> p a t i", i=2), ACT.Sigmoid,
+                logit[:, :, span].rearrange("p t (a i) -> p a t i", i=2),
+                ACT.Sigmoid,
             )
         for c in range(2):
             nc.vector.scalar_tensor_tensor(
-                z_bf[c][:], share[c][:], 2.0, gain[:].unsqueeze(1).to_broadcast([P, HALF, PACK]), ALU.mult, ALU.mult,
+                z_bf[c][:], share[c][:], 2.0, gain[:].unsqueeze(1).to_broadcast([P, HALF, SLOTS]), ALU.mult, ALU.mult
             )
-        for c in range(2):
-            nc.vector.quantize_mx(z_w[:, cols(c)].bitcast(FP8X4), z_s[:, cols(c)], z_bf[c][:].rearrange("p s t -> p (s t)"))
-            for t in range(PACK):
-                product(h_ps[t][:, cols(c)], w2w, w32s, 4, t, z_w[:, cols(c)], z_s[:, cols(c)])
+        for c, span in enumerate(halves):
+            nc.vector.quantize_mx(z_w[:, span].bitcast(FP8X4), z_s[:, span], z_bf[c][:].rearrange("p s t -> p (s t)"))
+            for t in range(SLOTS):
+                product(h_ps[t][:, span], w2w, w32s, W2_ROW, t, z_w[:, span], z_s[:, span])
 
-        wide.extend([sb("wide2", [P, 2 * S], F32, "logit"), sb("wide3", [P, 2 * S], F32, "share0")])
-        d_own.extend([wide[3][:, S:], wide[2][:, S:]])
+        d_win = dh_win + [sb("d_win2", [P, S], F32, reuses="logit"), sb("d_win3", [P, S], F32, reuses="share0")]
+        h_win = dh_win + [sb("h_win2", [P, S], F32), sb("h_win3", [P, S], F32)]
         for t in (2, 3):
-            nc.scalar.copy(wide[t][:, :S], d_ps[t][:])
-            nc.scalar.copy(d_own[t], d_ps[t][:])
-        d_first = sb("d_first", [P, 2, S], F32, tag="logs")
-        d_sum = [d_first[:, 0, :], d_first[:, 1, :], sb("d_sum2", [P, S], F32, tag="z_bf0")[:], sb("d_sum3", [P, S], F32, tag="z_bf1")[:]]
-        gate = sb("gate", [P, PACK, S], F32)
-        h_own = sb("h_own", [P, PACK, S], F32)
-        h_sum = sb("h_sum", [P, PACK, S], F32)
-        res = sb("res", [P, PACK, S], F32)
-        o_w = sb("o_w", [P, S], I32)
-        o_s = sb("o_s", [P, S], U8)
-        out_rows = out_0.rearrange("(p t) s -> p t s", t=PACK)
+            nc.scalar.copy(d_win[t][:], d_ps[t][:])
+        d_far01 = sb("d_far01", [P, 2, S], F32, reuses="logs")
+        d_far = [d_far01[:, 0, :], d_far01[:, 1, :]] + [sb(f"d_far{t}", [P, S], F32, reuses=f"z_bf{t - 2}")[:] for t in (2, 3)]
+        gate_turned = sb("gate_turned", [P, SLOTS, S], F32)
+        h_own = sb("h_own", [P, SLOTS, S], F32)
+        h_sum = sb("h_sum", [P, SLOTS, S], F32)
+        res = sb("res", [P, SLOTS, S], F32)
+        res_w = sb("res_w", [P, S], I32)
+        res_s = sb("res_s", [P, S], U8)
+        out_rows = out_0.rearrange("(p t) s -> p t s", t=SLOTS)
         out_words = out_1[0].rearrange("p c r -> p (c r)").bitcast(I32)
 
-        def gather_d(t):
-            nc.vector.tensor_tensor(d_sum[t], wide[t][:].indirect(n4_t[:]), d_own[t], ALU.add)
-
         def make_gate(t):
-            nc.scalar.activation(gate[:, t, :], d_sum[t], ACT.Sigmoid)
+            d_sum = turned_sum(f"d_sum{t}", f"hi{t}", d_win[t][:, :S], d_far[t])
+            nc.scalar.activation(gate_turned[:, t, :], d_sum[:], ACT.Sigmoid)
 
-        def copy_h(t):
-            nc.scalar.copy(wide[t][:, :S], h_ps[t][:])
-            nc.scalar.copy(h_own[:, t, :], h_ps[t][:])
+        def turn_gate(name, bank, slots, span):
+            width = span.stop - span.start
+            gate = psum.tile([P, len(slots), width], F32, name=name, tag=bank)
+            for j, t in enumerate(slots):
+                for lo in range(0, width, P):
+                    nc.tensor.transpose(gate[:, j, lo : lo + P], gate_turned[:, t, span.start + lo : span.start + lo + P], ident[:])
+            return gate
+
+        def copy_h(t, span):
+            nc.scalar.copy(h_win[t][:, :S], h_ps[t][:])
+            nc.scalar.copy(h_own[:, t, span], h_ps[t][:, span])
 
         def gather_h(t, span):
-            nc.vector.tensor_tensor(
-                h_sum[:, t, span], wide[t][:].indirect(n3_t[:, span.start // 16 : span.stop // 16]), h_own[:, t, span], ALU.add)
+            nc.vector.tensor_tensor(h_sum[:, t, span], h_win[t][:].indirect(entries(n3_t, span)), h_own[:, t, span], ALU.add)
 
-        def finish(slots, span):
-            nc.vector.tensor_tensor(res[:, slots, span], h_sum[:, slots, span], gate[:, slots, span], ALU.mult)
+        def finish(slots, span, gate):
+            nc.vector.tensor_tensor(res[:, slots, span], h_sum[:, slots, span], gate[:], ALU.mult)
             nc.sync.dma_start(out_rows[:, slots, span], res[:, slots, span])
 
-        def weave(engine_copy, c):
-            woven = sb(f"res_bf{c}", [P, HALF, PACK], BF16)
-            engine_copy(woven[:].rearrange("p (a i) t -> p a t i", i=4), res[:, :, cols(c)].rearrange("p t (a i) -> p a t i", i=4))
+        def weave(c, engine_copy):
+            woven = sb(f"res_bf{c}", [P, HALF, SLOTS], BF16)
+            engine_copy(
+                woven[:].rearrange("p (a i) t -> p a t i", i=4), res[:, :, halves[c]].rearrange("p t (a i) -> p a t i", i=4)
+            )
             return woven
 
-        def quantise(woven, c, queue):
-            nc.vector.quantize_mx(o_w[:, cols(c)].bitcast(FP8X4), o_s[:, cols(c)], woven[:].rearrange("p s t -> p (s t)"))
-            queue.dma_start(out_words[:, cols(c)], o_w[:, cols(c)])
+        def hand_on(c, woven, queue):
+            span = halves[c]
+            nc.vector.quantize_mx(res_w[:, span].bitcast(FP8X4), res_s[:, span], woven[:].rearrange("p s t -> p (s t)"))
+            queue.dma_start(out_words[:, span], res_w[:, span])
 
-        for t in range(PACK):
-            gather_d(t)
+        for t in (0, 1):
+            nc.vector.tensor_copy(d_far[t], d_win[t][:].indirect(n4_t[:]))
+        for t in (2, 3):
+            for span in halves:
+                nc.vector.tensor_copy(d_far[t][:, span], d_win[t][:].indirect(entries(n4_t, span)))
+
         make_gate(0)
         make_gate(1)
-        copy_h(0)
-        copy_h(1)
+        gate0 = turn_gate("gate0", "hi0", (0,), whole)
+        gate1 = turn_gate("gate1", "hi1", (1,), whole)
+        copy_h(0, whole)
+        copy_h(1, whole)
         make_gate(2)
-        copy_h(2)
+        copy_h(2, halves[0])
         make_gate(3)
-        copy_h(3)
-        whole = slice(0, S)
+        copy_h(3, halves[0])
+        for t in (2, 3):
+            nc.scalar.copy(h_own[:, t, halves[1]], h_ps[t][:, halves[1]])
+        gate23 = [turn_gate(f"gate23_{c}", f"hi{2 + c}", (2, 3), span) for c, span in enumerate(halves)]
         gather_h(0, whole)
         gather_h(1, whole)
-        finish(slice(0, 1), whole)
-        gather_h(2, cols(0))
-        finish(slice(1, 2), whole)
-        gather_h(3, cols(0))
-        gather_h(2, cols(1))
-        finish(slice(2, 4), cols(0))
-        first = weave(nc.scalar.copy, 0)
-        gather_h(3, cols(1))
-        finish(slice(2, 4), cols(1))
-        quantise(first, 0, nc.sync)
-        quantise(weave(nc.vector.tensor_copy, 1), 1, nc.scalar)
-        for q in range(4):
-            (nc.sync, nc.scalar)[q % 2].dma_start(out_2[0, 4 * q : 4 * q + 4, :].bitcast(I32), o_s[32 * q : 32 * q + 4, :].bitcast(I32))
+        finish(slice(0, 1), whole, gate0)
+        gather_h(2, halves[0])
+        finish(slice(1, 2), whole, gate1)
+        gather_h(3, halves[0])
+        gather_h(2, halves[1])
+        finish(slice(2, 4), halves[0], gate23[0])
+        woven_first = weave(0, nc.scalar.copy)
+        gather_h(3, halves[1])
+        finish(slice(2, 4), halves[1], gate23[1])
+        hand_on(0, woven_first, nc.sync)
+        hand_on(1, weave(1, nc.vector.tensor_copy), nc.scalar)
+        for q in range(P // QUADRANT):
+            (nc.sync, nc.scalar)[q % 2].dma_start(
+                out_2[0, 4 * q : 4 * q + 4, :].bitcast(I32), res_s[QUADRANT * q : QUADRANT * q + 4, :].bitcast(I32)
+            )

from contextlib import ExitStack

import concourse.mybir as mybir
from concourse.masks import make_identity

K, T, S, N, H = 512, 2048, 512, 512, 512
FLOPS = 2 * K * H * S + 2 * H * N * S + 2 * K * N * S

F32 = mybir.dt.float32
BF16 = mybir.dt.bfloat16
I32 = mybir.dt.int32
U32 = mybir.dt.uint32
U16 = mybir.dt.uint16
U8 = mybir.dt.uint8
FP8X4 = mybir.dt.float8_e4m3fn_x4
ACT = mybir.ActivationFunctionType
ALU = mybir.AluOpType

P = 128
SLOTS = 4
HALF = S // 2
GROUP = 16
QUADRANT = 32
W3_ROW, W2_ROW = 0, 4


def tile_picked_latetriebshare_none_po_kernel(
    tc, x_words, x_scales, w1_words, w1_scales, gn, w2_words, w2_scales, w3_words, w3_scales,
    offs, n1, n2, two, n3, n4, out_0, out_1, out_2,
):
    nc = tc.nc
    with ExitStack() as ctx:
        keep = ctx.enter_context(tc.tile_pool(name="keep", bufs=1))
        psum = ctx.enter_context(tc.psum_pool(name="psum", bufs=1))

        halves = (slice(0, HALF), slice(HALF, S))
        whole = slice(0, S)
        blocks = [slice(b * P, (b + 1) * P) for b in range(S // P)]

        def sb(name, shape, dtype, reuses=None):
            return keep.tile(shape, dtype, name=name, tag=reuses or name, align_bytes=64)

        def entries(lst, span):
            return lst[:, span.start // GROUP : span.stop // GROUP]

        def load_list(name, src):
            tile = sb(name, [P, S // GROUP], U16)
            nc.sync.dma_start(tile[:], src)
            return tile

        def load_words(queue, name, src, width):
            tile = sb(name, [P, width], I32)
            queue.dma_start(tile[:], src[0].rearrange("p c r -> p (c r)").bitcast(I32))
            return tile

        def load_scales(tile, first_row, src, queues):
            for q in range(P // QUADRANT):
                row = QUADRANT * q + first_row
                queues[q % 2].dma_start(tile[row : row + 4, :].bitcast(I32), src[0, 4 * q : 4 * q + 4, :].bitcast(I32))

        def deal_words(name, raw, reuses=None):
            tile = sb(name, [P, SLOTS, P], I32, reuses)
            nc.vector.tensor_copy(
                tile[:].rearrange("p t (a i) -> p a t i", i=4), raw[:].rearrange("p (a i t) -> p a t i", i=4, t=SLOTS)
            )
            return tile

        def deal_scales(name, raw):
            tile = sb(name, [P, SLOTS, P], U8)
            nc.vector.tensor_copy(tile[:], raw[:].rearrange("p (m t) -> p t m", t=SLOTS))
            return tile

        xs_raw = sb("xs_raw", [P, T], U8)
        w1s_raw = sb("w1s_raw", [P, H], U8)
        w32s_raw = sb("w32s_raw", [P, N], U8)
        nc.vector.memset(xs_raw[:, : T // 2].bitcast(I32), 0)
        nc.gpsimd.memset(xs_raw[:, T // 2 :].bitcast(I32), 0)
        for tile in (w1s_raw, w32s_raw):
            nc.gpsimd.memset(tile[:].bitcast(I32), 0)

        ident = sb("ident", [P, P], F32)
        make_identity(nc, ident[:])

        w1w_raw = load_words(nc.scalar, "w1w_raw", w1_words, H)
        offs_t = load_list("offs_t", offs)
        two_t = load_list("two_t", two)
        load_scales(xs_raw, 0, x_scales, (nc.sync, nc.scalar))
        xw_raw = load_words(nc.scalar, "xw_raw", x_words, T)
        load_scales(w1s_raw, 0, w1_scales, (nc.sync, nc.sync))
        w3w_raw = load_words(nc.sync, "w3w_raw", w3_words, N)
        load_scales(w32s_raw, W3_ROW, w3_scales, (nc.sync, nc.sync))
        load_scales(w32s_raw, W2_ROW, w2_scales, (nc.sync, nc.sync))
        n1_t = load_list("n1_t", n1)
        n2_t = load_list("n2_t", n2)
        n4_t = load_list("n4_t", n4)
        w2w_raw = load_words(nc.sync, "w2w_raw", w2_words, N)
        n3_t = load_list("n3_t", n3)
        gain = sb("gain", [P, SLOTS], F32)
        nc.sync.dma_start(gain[:], gn.rearrange("(p t) o -> p (t o)", t=SLOTS))

        def pick_scales(name, lst):
            tile = sb(name, [P, S], U8)
            nc.vector.tensor_copy(tile[:], xs_raw[:].indirect(lst[:]))
            return tile

        def pick_words(tile, lst):
            nc.vector.tensor_copy(tile[:].bitcast(U32), xw_raw[:].bitcast(U32).indirect(lst[:]))

        xa_s = pick_scales("xa_s", offs_t)
        w1w = deal_words("w1w", w1w_raw)
        xb_s = pick_scales("xb_s", two_t)
        xa_w = sb("xa_w", [P, S], I32)
        xb_w = sb("xb_w", [P, S], I32, reuses="w1s_raw")
        pick_words(xa_w, offs_t)
        w1s = deal_scales("w1s", w1s_raw)
        pick_words(xb_w, two_t)
        w3w = deal_words("w3w", w3w_raw)
        w32s = deal_scales("w32s", w32s_raw)

        def product(out, w_words, w_scales, first_row, t, words, scales):
            nc.tensor.matmul_mx(
                out=out, lhsT=w_words[:, t, :].bitcast(FP8X4), lhsT_scale=w_scales[first_row:P, t, :],
                rhs=words.bitcast(FP8X4), rhs_scale=scales, start=True, stop=True,
            )

        y_ps = [psum.tile([P, S], F32, name=f"y_ps{t}", tag=f"lo{t}") for t in range(SLOTS)]
        d_ps = [psum.tile([P, S], F32, name=f"d_ps{t}", tag=f"hi{t}") for t in range(SLOTS)]
        for t in range(SLOTS):
            product(y_ps[t][:], w1w, w1s, 0, t, xa_w[:], xa_s[:])
        for t in range(SLOTS):
            product(d_ps[t][:], w3w, w32s, W3_ROW, t, xb_w[:], xb_s[:])

        ex0 = sb("ex0", [P, S], F32)
        ex1 = sb("ex1", [P, 2 * S], F32)
        ex2 = sb("ex2", [P, 2 * S], F32)
        y3 = sb("y3", [P, S], F32)
        dh_win = [sb(f"dh_win{t}", [P, 2 * S], F32) for t in (0, 1)]
        near = [ex1[:, S:], dh_win[0][:, S:], dh_win[1][:, S:], sb("near3", [P, S], F32)[:]]
        far3 = sb("far3", [P, S], F32)
        pair = [ex2[:, S:]] + [sb(f"pair{t}", [P, S], F32)[:] for t in (1, 2)]
        for t, win in enumerate((ex0, ex1, ex2)):
            nc.scalar.activation(win[:, :S], y_ps[t][:], ACT.Exp, scale=0.5)
        nc.scalar.copy(y3[:], y_ps[3][:])
        for dst, lst in ((near[3], n1_t), (far3[:], n2_t)):
            for span in halves:
                nc.scalar.activation(dst[:, span], y3[:].indirect(entries(lst, span)), ACT.Exp, scale=0.5)
        for span in halves:
            nc.vector.tensor_copy(near[0][:, span], ex0[:].indirect(entries(n1_t, span)))
        for span in halves:
            nc.vector.tensor_tensor(pair[0][:, span], ex0[:].indirect(entries(n2_t, span)), near[0][:, span], ALU.add)
        for t, win in ((1, ex1), (2, ex2)):
            nc.vector.tensor_copy(near[t], win[:].indirect(n1_t[:]))
        for t, win in ((1, ex1), (2, ex2)):
            nc.vector.tensor_tensor(pair[t], win[:].indirect(n2_t[:]), near[t], ALU.add)

        def turned_sum(name, bank, first, second):
            acc = psum.tile([P, S], F32, name=name, tag=bank)
            for blk in blocks:
                nc.tensor.matmul(acc[:, blk], first[:, blk], ident[:], start=True, stop=False, is_transpose=True)
                nc.tensor.matmul(acc[:, blk], second[:, blk], ident[:], start=False, stop=True, is_transpose=True)
            return acc

        pair3_ps = turned_sum("pair3_ps", "lo3", near[3], far3[:])

        w2w = deal_words("w2w", w2w_raw, reuses="ex1")
        for t in (0, 1):
            nc.scalar.copy(dh_win[t][:, :S], d_ps[t][:])

        logs = sb("logs", [P, 3, S], F32)
        logit = sb("logit", [P, SLOTS, S], F32)
        log3_turned = sb("log3_turned", [P, S], F32)
        nc.scalar.activation(log3_turned[:], pair3_ps[:], ACT.Ln)
        log3_ps = psum.tile([P, S], F32, name="log3_ps", tag="lo3")
        for blk in blocks:
            nc.tensor.transpose(log3_ps[:, blk], log3_turned[:, blk], ident[:])
        nc.vector.scalar_tensor_tensor(logit[:, 3, :], y3[:], 0.5, log3_ps[:], ALU.mult, ALU.subtract)
        for t in range(3):
            nc.scalar.activation(logs[:, t, :], pair[t], ACT.Ln)
            nc.vector.scalar_tensor_tensor(logit[:, t, :], y_ps[t][:], 0.5, logs[:, t, :], ALU.mult, ALU.subtract)

        share = [sb(f"share{c}", [P, HALF, SLOTS], F32) for c in range(2)]
        z_bf = [sb(f"z_bf{c}", [P, HALF, SLOTS], BF16) for c in range(2)]
        z_w = sb("z_w", [P, S], I32)
        z_s = sb("z_s", [P, S], U8)
        h_ps = [psum.tile([P, S], F32, name=f"h_ps{t}", tag=f"lo{t}") for t in range(SLOTS)]
        for c, span in enumerate(halves):
            nc.scalar.activation(
                share[c][:].rearrange("p (a i) t -> p a t i", i=2),
                logit[:, :, span].rearrange("p t (a i) -> p a t i", i=2),
                ACT.Sigmoid,
            )
        for c in range(2):
            nc.vector.scalar_tensor_tensor(
                z_bf[c][:], share[c][:], 2.0, gain[:].unsqueeze(1).to_broadcast([P, HALF, SLOTS]), ALU.mult, ALU.mult
            )
        for c, span in enumerate(halves):
            nc.vector.quantize_mx(z_w[:, span].bitcast(FP8X4), z_s[:, span], z_bf[c][:].rearrange("p s t -> p (s t)"))
            for t in range(SLOTS):
                product(h_ps[t][:, span], w2w, w32s, W2_ROW, t, z_w[:, span], z_s[:, span])

        d_win = dh_win + [sb("d_win2", [P, S], F32, reuses="logit"), sb("d_win3", [P, S], F32, reuses="share0")]
        h_win = dh_win + [sb("h_win2", [P, S], F32), sb("h_win3", [P, S], F32)]
        for t in (2, 3):
            nc.scalar.copy(d_win[t][:], d_ps[t][:])
        d_far01 = sb("d_far01", [P, 2, S], F32, reuses="logs")
        d_far = [d_far01[:, 0, :], d_far01[:, 1, :]] + [sb(f"d_far{t}", [P, S], F32, reuses=f"z_bf{t - 2}")[:] for t in (2, 3)]
        gate_turned = sb("gate_turned", [P, SLOTS, S], F32)
        h_own = sb("h_own", [P, SLOTS, S], F32)
        h_sum = sb("h_sum", [P, SLOTS, S], F32)
        res = sb("res", [P, SLOTS, S], F32)
        res_w = sb("res_w", [P, S], I32)
        res_s = sb("res_s", [P, S], U8)
        out_rows = out_0.rearrange("(p t) s -> p t s", t=SLOTS)
        out_words = out_1[0].rearrange("p c r -> p (c r)").bitcast(I32)

        def make_gate(t):
            d_sum = turned_sum(f"d_sum{t}", f"hi{t}", d_win[t][:, :S], d_far[t])
            nc.scalar.activation(gate_turned[:, t, :], d_sum[:], ACT.Sigmoid)

        def turn_gate(name, bank, slots, span):
            width = span.stop - span.start
            gate = psum.tile([P, len(slots), width], F32, name=name, tag=bank)
            for j, t in enumerate(slots):
                for lo in range(0, width, P):
                    nc.tensor.transpose(gate[:, j, lo : lo + P], gate_turned[:, t, span.start + lo : span.start + lo + P], ident[:])
            return gate

        def copy_h(t, span):
            nc.scalar.copy(h_win[t][:, :S], h_ps[t][:])
            nc.scalar.copy(h_own[:, t, span], h_ps[t][:, span])

        def gather_h(t, span):
            nc.vector.tensor_tensor(h_sum[:, t, span], h_win[t][:].indirect(entries(n3_t, span)), h_own[:, t, span], ALU.add)

        def finish(slots, span, gate):
            nc.vector.tensor_tensor(res[:, slots, span], h_sum[:, slots, span], gate[:], ALU.mult)
            nc.sync.dma_start(out_rows[:, slots, span], res[:, slots, span])

        def weave(c, engine_copy):
            woven = sb(f"res_bf{c}", [P, HALF, SLOTS], BF16)
            engine_copy(
                woven[:].rearrange("p (a i) t -> p a t i", i=4), res[:, :, halves[c]].rearrange("p t (a i) -> p a t i", i=4)
            )
            return woven

        def hand_on(c, woven, queue):
            span = halves[c]
            nc.vector.quantize_mx(res_w[:, span].bitcast(FP8X4), res_s[:, span], woven[:].rearrange("p s t -> p (s t)"))
            queue.dma_start(out_words[:, span], res_w[:, span])

        for t in (0, 1):
            nc.vector.tensor_copy(d_far[t], d_win[t][:].indirect(n4_t[:]))
        for t in (2, 3):
            for span in halves:
                nc.vector.tensor_copy(d_far[t][:, span], d_win[t][:].indirect(entries(n4_t, span)))

        make_gate(0)
        make_gate(1)
        gate0 = turn_gate("gate0", "hi0", (0,), whole)
        gate1 = turn_gate("gate1", "hi1", (1,), whole)
        copy_h(0, whole)
        copy_h(1, whole)
        make_gate(2)
        copy_h(2, halves[0])
        make_gate(3)
        copy_h(3, halves[0])
        for t in (2, 3):
            nc.scalar.copy(h_own[:, t, halves[1]], h_ps[t][:, halves[1]])
        gate23 = [turn_gate(f"gate23_{c}", f"hi{2 + c}", (2, 3), span) for c, span in enumerate(halves)]
        gather_h(0, whole)
        gather_h(1, whole)
        finish(slice(0, 1), whole, gate0)
        gather_h(2, halves[0])
        finish(slice(1, 2), whole, gate1)
        gather_h(3, halves[0])
        gather_h(2, halves[1])
        finish(slice(2, 4), halves[0], gate23[0])
        woven_first = weave(0, nc.scalar.copy)
        gather_h(3, halves[1])
        finish(slice(2, 4), halves[1], gate23[1])
        hand_on(0, woven_first, nc.sync)
        hand_on(1, weave(1, nc.vector.tensor_copy), nc.scalar)
        for q in range(P // QUADRANT):
            (nc.sync, nc.scalar)[q % 2].dma_start(
                out_2[0, 4 * q : 4 * q + 4, :].bitcast(I32), res_s[QUADRANT * q : QUADRANT * q + 4, :].bitcast(I32)
            )
